import numpy as np
CORES = [2,130,258,386]
N = 4
def setup_inputs(rng):
    return {"x": rng.standard_normal((N, 128, 64), dtype=np.float32)}
def reference(x):
    g = np.concatenate(list(x), axis=1)
    return {"y": np.broadcast_to(g, (N,) + g.shape)}

@@ -1,0 +1,75 @@
+from concourse.bass import DstId, RemoteDMATransfer
+
+SCRATCH = {
+    "own": ("dram", [2, 128, 32], "float32"),
+    "relay": ("dram", [128, 32], "float32"),
+    "nbl": ("dram", [2, 128, 32], "float32"),
+    "nbr": ("dram", [2, 128, 32], "float32"),
+    "dg": ("dram", [2, 128, 32], "float32"),
+}
+SEMAPHORES = ["loaded", "sent", "relay", "nbl", "nbr", "dgt", "dgb", "stored"]
+
+FWD_UP, FWD_DOWN = 6, 4
+W = 64
+
+
+def rank_program(g, core, T, topo):
+    cores = list(T.cores)
+    n = len(cores)
+    s = T.sem
+    rank = T.rank_of(core)
+
+    if rank is None:
+        q = None
+        for i in range(n):
+            if cores[i] // 8 == core // 8:
+                q = i
+        if q is None or core % 8 not in (FWD_UP, FWD_DOWN):
+            return
+        up = core % 8 == FWD_UP
+        dst = cores[(q + 1) % n] if up else cores[(q - 1) % n]
+        rid, pid = topo.addr(dst, core)
+        g.wait_ge(s.relay, 4)
+        g.remote_dma(T.dg[0 if up else 1], T.relay[:], s.dgt if up else s.dgb, s.sent, pid, rid, 0xFF)
+        g.wait_ge(s.sent, 8)
+        return
+
+    nxt, prv = cores[(rank + 1) % n], cores[(rank - 1) % n]
+
+    def did(dst):
+        rid, pid = topo.addr(dst, core)
+        return DstId(rid=rid, pnc=pid)
+
+    def col(j):
+        return slice(W * (j % n), W * (j % n) + W)
+
+    g.sync.dma_start(T.own[:], T.x[:]).then_inc(s.loaded, 16)
+    g.wait_ge(s.loaded, 16)
+
+    g.remote_dma_fused([
+        RemoteDMATransfer(dst_ids=[did(nxt - nxt % 8 + FWD_UP)], dma_engine_mask=0x0F, remote_sem=s.relay,
+                          src=T.own[0], dst=T.relay[:]),
+        RemoteDMATransfer(dst_ids=[did(prv - prv % 8 + FWD_DOWN)], dma_engine_mask=0xF0, remote_sem=s.relay,
+                          src=T.own[1], dst=T.relay[:]),
+    ], local_sem=s.sent)
+    g.remote_dma_fused([
+        RemoteDMATransfer(dst_ids=[did(nxt)], dma_engine_mask=0x03, remote_sem=s.nbl, src=T.own[0], dst=T.nbl[0]),
+        RemoteDMATransfer(dst_ids=[did(nxt)], dma_engine_mask=0x0C, remote_sem=s.nbl, src=T.own[1], dst=T.nbl[1]),
+        RemoteDMATransfer(dst_ids=[did(prv)], dma_engine_mask=0x30, remote_sem=s.nbr, src=T.own[0], dst=T.nbr[0]),
+        RemoteDMATransfer(dst_ids=[did(prv)], dma_engine_mask=0xC0, remote_sem=s.nbr, src=T.own[1], dst=T.nbr[1]),
+    ], local_sem=s.sent)
+
+    g.sync.wait_ge(s.nbl, 4)
+    g.sync.dma_start(T.y[:, col(rank - 1)], T.nbl[:]).then_inc(s.stored, 16)
+    g.sync.wait_ge(s.dgt, 8)
+    g.sync.dma_start(T.y[0:64, col(rank + 2)], T.dg[0]).then_inc(s.stored, 16)
+
+    g.scalar.wait_ge(s.sent, 16)
+    g.scalar.dma_start(T.y[:, col(rank)], T.x[:]).then_inc(s.stored, 16)
+    g.scalar.wait_ge(s.nbr, 4)
+    g.scalar.dma_start(T.y[:, col(rank + 1)], T.nbr[:]).then_inc(s.stored, 16)
+    g.scalar.wait_ge(s.dgb, 8)
+    g.scalar.dma_start(T.y[64:128, col(rank + 2)], T.dg[1]).then_inc(s.stored, 16)
+
+    g.wait_ge(s.sent, 16)
+    g.wait_ge(s.stored, 80)

@@ -7,7 +7,7 @@ SCRATCH = {
     "nbr": ("dram", [2, 128, 32], "float32"),
     "dg": ("dram", [2, 128, 32], "float32"),
 }
-SEMAPHORES = ["loaded", "sent", "relay", "nbl", "nbr", "dgt", "dgb", "stored"]
+SEMAPHORES = ["loaded", "sent", "relay", "nbld", "nblf", "nbrd", "nbrf", "dgt", "dgb", "stored"]
 
 FWD_UP, FWD_DOWN = 6, 4
 W = 64
@@ -19,6 +19,10 @@ def rank_program(g, core, T, topo):
     s = T.sem
     rank = T.rank_of(core)
 
+    def did(dst):
+        rid, pid = topo.addr(dst, core)
+        return DstId(rid=rid, pnc=pid)
+
     if rank is None:
         q = None
         for i in range(n):
@@ -28,17 +32,17 @@ def rank_program(g, core, T, topo):
             return
         up = core % 8 == FWD_UP
         dst = cores[(q + 1) % n] if up else cores[(q - 1) % n]
-        rid, pid = topo.addr(dst, core)
         g.wait_ge(s.relay, 4)
-        g.remote_dma(T.dg[0 if up else 1], T.relay[:], s.dgt if up else s.dgb, s.sent, pid, rid, 0xFF)
-        g.wait_ge(s.sent, 8)
+        g.remote_dma_fused([
+            RemoteDMATransfer(dst_ids=[did(dst)], dma_engine_mask=0x00FF, remote_sem=s.dgt if up else s.dgb,
+                              src=T.relay[:], dst=T.dg[0 if up else 1]),
+            RemoteDMATransfer(dst_ids=[did(cores[q])], dma_engine_mask=0xFF00, remote_sem=s.nblf if up else s.nbrf,
+                              src=T.relay[:], dst=T.nbl[0] if up else T.nbr[1]),
+        ], local_sem=s.sent)
+        g.wait_ge(s.sent, 16)
         return
 
     nxt, prv = cores[(rank + 1) % n], cores[(rank - 1) % n]
-
-    def did(dst):
-        rid, pid = topo.addr(dst, core)
-        return DstId(rid=rid, pnc=pid)
 
     def col(j):
         return slice(W * (j % n), W * (j % n) + W)
@@ -53,23 +57,25 @@ def rank_program(g, core, T, topo):
                           src=T.own[1], dst=T.relay[:]),
     ], local_sem=s.sent)
     g.remote_dma_fused([
-        RemoteDMATransfer(dst_ids=[did(nxt)], dma_engine_mask=0x03, remote_sem=s.nbl, src=T.own[0], dst=T.nbl[0]),
-        RemoteDMATransfer(dst_ids=[did(nxt)], dma_engine_mask=0x0C, remote_sem=s.nbl, src=T.own[1], dst=T.nbl[1]),
-        RemoteDMATransfer(dst_ids=[did(prv)], dma_engine_mask=0x30, remote_sem=s.nbr, src=T.own[0], dst=T.nbr[0]),
-        RemoteDMATransfer(dst_ids=[did(prv)], dma_engine_mask=0xC0, remote_sem=s.nbr, src=T.own[1], dst=T.nbr[1]),
+        RemoteDMATransfer(dst_ids=[did(nxt)], dma_engine_mask=0x0F, remote_sem=s.nbld, src=T.own[1], dst=T.nbl[1]),
+        RemoteDMATransfer(dst_ids=[did(prv)], dma_engine_mask=0xF0, remote_sem=s.nbrd, src=T.own[0], dst=T.nbr[0]),
     ], local_sem=s.sent)
 
-    g.sync.wait_ge(s.nbl, 4)
-    g.sync.dma_start(T.y[:, col(rank - 1)], T.nbl[:]).then_inc(s.stored, 16)
+    g.sync.wait_ge(s.nbld, 4)
+    g.sync.dma_start(T.y[64:128, col(rank - 1)], T.nbl[1]).then_inc(s.stored, 16)
+    g.sync.wait_ge(s.nblf, 8)
+    g.sync.dma_start(T.y[0:64, col(rank - 1)], T.nbl[0]).then_inc(s.stored, 16)
     g.sync.wait_ge(s.dgt, 8)
     g.sync.dma_start(T.y[0:64, col(rank + 2)], T.dg[0]).then_inc(s.stored, 16)
 
     g.scalar.wait_ge(s.sent, 16)
     g.scalar.dma_start(T.y[:, col(rank)], T.x[:]).then_inc(s.stored, 16)
-    g.scalar.wait_ge(s.nbr, 4)
-    g.scalar.dma_start(T.y[:, col(rank + 1)], T.nbr[:]).then_inc(s.stored, 16)
+    g.scalar.wait_ge(s.nbrd, 4)
+    g.scalar.dma_start(T.y[0:64, col(rank + 1)], T.nbr[0]).then_inc(s.stored, 16)
+    g.scalar.wait_ge(s.nbrf, 8)
+    g.scalar.dma_start(T.y[64:128, col(rank + 1)], T.nbr[1]).then_inc(s.stored, 16)
     g.scalar.wait_ge(s.dgb, 8)
     g.scalar.dma_start(T.y[64:128, col(rank + 2)], T.dg[1]).then_inc(s.stored, 16)
 
     g.wait_ge(s.sent, 16)
-    g.wait_ge(s.stored, 80)
+    g.wait_ge(s.stored, 112)

@@ -1,16 +1,25 @@
 from concourse.bass import DstId, RemoteDMATransfer
 
 SCRATCH = {
-    "own": ("dram", [2, 128, 32], "float32"),
-    "relay": ("dram", [128, 32], "float32"),
-    "nbl": ("dram", [2, 128, 32], "float32"),
-    "nbr": ("dram", [2, 128, 32], "float32"),
-    "dg": ("dram", [2, 128, 32], "float32"),
+    "own": ("dram", [4, 128, 16], "float32"),
+    "relay": ("dram", [128, 16], "float32"),
+    "nbl": ("dram", [4, 128, 16], "float32"),
+    "nbr": ("dram", [4, 128, 16], "float32"),
+    "dg": ("dram", [4, 128, 16], "float32"),
 }
 SEMAPHORES = ["loaded", "sent", "relay", "nbld", "nblf", "nbrd", "nbrf", "dgt", "dgb", "stored"]
 
-FWD_UP, FWD_DOWN = 6, 4
+CABLE_FWD = (4, 6)
+SWITCH_FWD = (5, 1)
 W = 64
+
+
+def fwd_cores(topo, cores, q, step):
+    n = len(cores)
+    a, b = topo.host(cores[q]), topo.host(cores[(q + step) % n])
+    loc = SWITCH_FWD if topo.rack(a) == topo.rack(b) else CABLE_FWD
+    base = cores[q] - cores[q] % 8
+    return [base + loc[0], base + loc[1]]
 
 
 def rank_program(g, core, T, topo):
@@ -28,21 +37,29 @@ def rank_program(g, core, T, topo):
         for i in range(n):
             if cores[i] // 8 == core // 8:
                 q = i
-        if q is None or core % 8 not in (FWD_UP, FWD_DOWN):
+        if q is None:
             return
-        up = core % 8 == FWD_UP
+        ups, downs = fwd_cores(topo, cores, q, 1), fwd_cores(topo, cores, q, -1)
+        if core in ups:
+            up, p = True, ups.index(core)
+        elif core in downs:
+            up, p = False, 2 + downs.index(core)
+        else:
+            return
         dst = cores[(q + 1) % n] if up else cores[(q - 1) % n]
-        g.wait_ge(s.relay, 4)
+        g.wait_ge(s.relay, 2)
         g.remote_dma_fused([
             RemoteDMATransfer(dst_ids=[did(dst)], dma_engine_mask=0x00FF, remote_sem=s.dgt if up else s.dgb,
-                              src=T.relay[:], dst=T.dg[0 if up else 1]),
+                              src=T.relay[:], dst=T.dg[p]),
             RemoteDMATransfer(dst_ids=[did(cores[q])], dma_engine_mask=0xFF00, remote_sem=s.nblf if up else s.nbrf,
-                              src=T.relay[:], dst=T.nbl[0] if up else T.nbr[1]),
+                              src=T.relay[:], dst=T.nbl[p] if up else T.nbr[p]),
         ], local_sem=s.sent)
         g.wait_ge(s.sent, 16)
         return
 
     nxt, prv = cores[(rank + 1) % n], cores[(rank - 1) % n]
+    f_up = fwd_cores(topo, cores, (rank + 1) % n, 1)
+    f_dn = fwd_cores(topo, cores, (rank - 1) % n, -1)
 
     def col(j):
         return slice(W * (j % n), W * (j % n) + W)
@@ -51,31 +68,33 @@ def rank_program(g, core, T, topo):
     g.wait_ge(s.loaded, 16)
 
     g.remote_dma_fused([
-        RemoteDMATransfer(dst_ids=[did(nxt - nxt % 8 + FWD_UP)], dma_engine_mask=0x0F, remote_sem=s.relay,
-                          src=T.own[0], dst=T.relay[:]),
-        RemoteDMATransfer(dst_ids=[did(prv - prv % 8 + FWD_DOWN)], dma_engine_mask=0xF0, remote_sem=s.relay,
-                          src=T.own[1], dst=T.relay[:]),
+        RemoteDMATransfer(dst_ids=[did(f_up[0])], dma_engine_mask=0x03, remote_sem=s.relay, src=T.own[0], dst=T.relay[:]),
+        RemoteDMATransfer(dst_ids=[did(f_up[1])], dma_engine_mask=0x0C, remote_sem=s.relay, src=T.own[1], dst=T.relay[:]),
+        RemoteDMATransfer(dst_ids=[did(f_dn[0])], dma_engine_mask=0x30, remote_sem=s.relay, src=T.own[2], dst=T.relay[:]),
+        RemoteDMATransfer(dst_ids=[did(f_dn[1])], dma_engine_mask=0xC0, remote_sem=s.relay, src=T.own[3], dst=T.relay[:]),
     ], local_sem=s.sent)
     g.remote_dma_fused([
-        RemoteDMATransfer(dst_ids=[did(nxt)], dma_engine_mask=0x0F, remote_sem=s.nbld, src=T.own[1], dst=T.nbl[1]),
-        RemoteDMATransfer(dst_ids=[did(prv)], dma_engine_mask=0xF0, remote_sem=s.nbrd, src=T.own[0], dst=T.nbr[0]),
+        RemoteDMATransfer(dst_ids=[did(nxt)], dma_engine_mask=0x03, remote_sem=s.nbld, src=T.own[2], dst=T.nbl[2]),
+        RemoteDMATransfer(dst_ids=[did(nxt)], dma_engine_mask=0x0C, remote_sem=s.nbld, src=T.own[3], dst=T.nbl[3]),
+        RemoteDMATransfer(dst_ids=[did(prv)], dma_engine_mask=0x30, remote_sem=s.nbrd, src=T.own[0], dst=T.nbr[0]),
+        RemoteDMATransfer(dst_ids=[did(prv)], dma_engine_mask=0xC0, remote_sem=s.nbrd, src=T.own[1], dst=T.nbr[1]),
     ], local_sem=s.sent)
 
     g.sync.wait_ge(s.nbld, 4)
-    g.sync.dma_start(T.y[64:128, col(rank - 1)], T.nbl[1]).then_inc(s.stored, 16)
-    g.sync.wait_ge(s.nblf, 8)
-    g.sync.dma_start(T.y[0:64, col(rank - 1)], T.nbl[0]).then_inc(s.stored, 16)
-    g.sync.wait_ge(s.dgt, 8)
-    g.sync.dma_start(T.y[0:64, col(rank + 2)], T.dg[0]).then_inc(s.stored, 16)
+    g.sync.dma_start(T.y[64:128, col(rank - 1)], T.nbl[2:4]).then_inc(s.stored, 16)
+    g.sync.wait_ge(s.nblf, 16)
+    g.sync.dma_start(T.y[0:64, col(rank - 1)], T.nbl[0:2]).then_inc(s.stored, 16)
+    g.sync.wait_ge(s.dgt, 16)
+    g.sync.dma_start(T.y[0:64, col(rank + 2)], T.dg[0:2]).then_inc(s.stored, 16)
 
     g.scalar.wait_ge(s.sent, 16)
     g.scalar.dma_start(T.y[:, col(rank)], T.x[:]).then_inc(s.stored, 16)
     g.scalar.wait_ge(s.nbrd, 4)
-    g.scalar.dma_start(T.y[0:64, col(rank + 1)], T.nbr[0]).then_inc(s.stored, 16)
-    g.scalar.wait_ge(s.nbrf, 8)
-    g.scalar.dma_start(T.y[64:128, col(rank + 1)], T.nbr[1]).then_inc(s.stored, 16)
-    g.scalar.wait_ge(s.dgb, 8)
-    g.scalar.dma_start(T.y[64:128, col(rank + 2)], T.dg[1]).then_inc(s.stored, 16)
+    g.scalar.dma_start(T.y[0:64, col(rank + 1)], T.nbr[0:2]).then_inc(s.stored, 16)
+    g.scalar.wait_ge(s.nbrf, 16)
+    g.scalar.dma_start(T.y[64:128, col(rank + 1)], T.nbr[2:4]).then_inc(s.stored, 16)
+    g.scalar.wait_ge(s.dgb, 16)
+    g.scalar.dma_start(T.y[64:128, col(rank + 2)], T.dg[2:4]).then_inc(s.stored, 16)
 
     g.wait_ge(s.sent, 16)
     g.wait_ge(s.stored, 112)

@@ -3,23 +3,15 @@ from concourse.bass import DstId, RemoteDMATransfer
 SCRATCH = {
     "own": ("dram", [4, 128, 16], "float32"),
     "relay": ("dram", [128, 16], "float32"),
-    "nbl": ("dram", [4, 128, 16], "float32"),
-    "nbr": ("dram", [4, 128, 16], "float32"),
+    "nsw": ("dram", [4, 128, 16], "float32"),
+    "ncb": ("dram", [4, 128, 16], "float32"),
     "dg": ("dram", [4, 128, 16], "float32"),
 }
-SEMAPHORES = ["loaded", "sent", "relay", "nbld", "nblf", "nbrd", "nbrf", "dgt", "dgb", "stored"]
+SEMAPHORES = ["loaded", "sent", "relay", "nswd", "nswf", "ncbd", "ncbf", "dga", "dgb", "stored"]
 
-CABLE_FWD = (4, 6)
-SWITCH_FWD = (5, 1)
+CABLE_FWD = (4, 6, 0)
+SWITCH_FWD = 5
 W = 64
-
-
-def fwd_cores(topo, cores, q, step):
-    n = len(cores)
-    a, b = topo.host(cores[q]), topo.host(cores[(q + step) % n])
-    loc = SWITCH_FWD if topo.rack(a) == topo.rack(b) else CABLE_FWD
-    base = cores[q] - cores[q] % 8
-    return [base + loc[0], base + loc[1]]
 
 
 def rank_program(g, core, T, topo):
@@ -32,6 +24,15 @@ def rank_program(g, core, T, topo):
         rid, pid = topo.addr(dst, core)
         return DstId(rid=rid, pnc=pid)
 
+    def tr(dst, mask, sem, src, out):
+        return RemoteDMATransfer(dst_ids=[did(dst)], dma_engine_mask=mask, remote_sem=sem, src=src, dst=out)
+
+    def neighbours(q):
+        a, b = (q + 1) % n, (q - 1) % n
+        if topo.rack(topo.host(cores[a])) == topo.rack(topo.host(cores[q])):
+            return a, b
+        return b, a
+
     if rank is None:
         q = None
         for i in range(n):
@@ -39,62 +40,62 @@ def rank_program(g, core, T, topo):
                 q = i
         if q is None:
             return
-        ups, downs = fwd_cores(topo, cores, q, 1), fwd_cores(topo, cores, q, -1)
-        if core in ups:
-            up, p = True, ups.index(core)
-        elif core in downs:
-            up, p = False, 2 + downs.index(core)
-        else:
+        sw, cb = neighbours(q)
+        loc = core % 8
+        g_calls = None
+        if loc in CABLE_FWD:
+            p = CABLE_FWD.index(loc)
+            g_calls = [tr(cores[cb], 0x00FF, s.dga, T.relay[:], T.dg[p]),
+                       tr(cores[q], 0xFF00, s.nswf, T.relay[:], T.nsw[p])]
+        elif loc == SWITCH_FWD:
+            g_calls = [tr(cores[sw], 0x00FF, s.dgb, T.relay[:], T.dg[3]),
+                       tr(cores[q], 0xFF00, s.ncbf, T.relay[:], T.ncb[3])]
+        if g_calls is None:
             return
-        dst = cores[(q + 1) % n] if up else cores[(q - 1) % n]
         g.wait_ge(s.relay, 2)
-        g.remote_dma_fused([
-            RemoteDMATransfer(dst_ids=[did(dst)], dma_engine_mask=0x00FF, remote_sem=s.dgt if up else s.dgb,
-                              src=T.relay[:], dst=T.dg[p]),
-            RemoteDMATransfer(dst_ids=[did(cores[q])], dma_engine_mask=0xFF00, remote_sem=s.nblf if up else s.nbrf,
-                              src=T.relay[:], dst=T.nbl[p] if up else T.nbr[p]),
-        ], local_sem=s.sent)
+        g.remote_dma_fused(g_calls, local_sem=s.sent)
         g.wait_ge(s.sent, 16)
         return
 
-    nxt, prv = cores[(rank + 1) % n], cores[(rank - 1) % n]
-    f_up = fwd_cores(topo, cores, (rank + 1) % n, 1)
-    f_dn = fwd_cores(topo, cores, (rank - 1) % n, -1)
+    sw, cb = neighbours(rank)
+    dgr = (rank + 2) % n
+    csw, ccb = cores[sw], cores[cb]
+    bsw, bcb = csw - csw % 8, ccb - ccb % 8
 
     def col(j):
-        return slice(W * (j % n), W * (j % n) + W)
+        return slice(W * j, W * j + W)
 
     g.sync.dma_start(T.own[:], T.x[:]).then_inc(s.loaded, 16)
     g.wait_ge(s.loaded, 16)
 
     g.remote_dma_fused([
-        RemoteDMATransfer(dst_ids=[did(f_up[0])], dma_engine_mask=0x03, remote_sem=s.relay, src=T.own[0], dst=T.relay[:]),
-        RemoteDMATransfer(dst_ids=[did(f_up[1])], dma_engine_mask=0x0C, remote_sem=s.relay, src=T.own[1], dst=T.relay[:]),
-        RemoteDMATransfer(dst_ids=[did(f_dn[0])], dma_engine_mask=0x30, remote_sem=s.relay, src=T.own[2], dst=T.relay[:]),
-        RemoteDMATransfer(dst_ids=[did(f_dn[1])], dma_engine_mask=0xC0, remote_sem=s.relay, src=T.own[3], dst=T.relay[:]),
+        tr(bsw + CABLE_FWD[0], 0x03, s.relay, T.own[0], T.relay[:]),
+        tr(bsw + CABLE_FWD[1], 0x0C, s.relay, T.own[1], T.relay[:]),
+        tr(bsw + CABLE_FWD[2], 0x30, s.relay, T.own[2], T.relay[:]),
+        tr(bcb + SWITCH_FWD, 0xC0, s.relay, T.own[3], T.relay[:]),
     ], local_sem=s.sent)
     g.remote_dma_fused([
-        RemoteDMATransfer(dst_ids=[did(nxt)], dma_engine_mask=0x03, remote_sem=s.nbld, src=T.own[2], dst=T.nbl[2]),
-        RemoteDMATransfer(dst_ids=[did(nxt)], dma_engine_mask=0x0C, remote_sem=s.nbld, src=T.own[3], dst=T.nbl[3]),
-        RemoteDMATransfer(dst_ids=[did(prv)], dma_engine_mask=0x30, remote_sem=s.nbrd, src=T.own[0], dst=T.nbr[0]),
-        RemoteDMATransfer(dst_ids=[did(prv)], dma_engine_mask=0xC0, remote_sem=s.nbrd, src=T.own[1], dst=T.nbr[1]),
+        tr(ccb, 0x03, s.ncbd, T.own[0], T.ncb[0]),
+        tr(ccb, 0x0C, s.ncbd, T.own[1], T.ncb[1]),
+        tr(ccb, 0x30, s.ncbd, T.own[2], T.ncb[2]),
+        tr(csw, 0xC0, s.nswd, T.own[3], T.nsw[3]),
     ], local_sem=s.sent)
 
-    g.sync.wait_ge(s.nbld, 4)
-    g.sync.dma_start(T.y[64:128, col(rank - 1)], T.nbl[2:4]).then_inc(s.stored, 16)
-    g.sync.wait_ge(s.nblf, 16)
-    g.sync.dma_start(T.y[0:64, col(rank - 1)], T.nbl[0:2]).then_inc(s.stored, 16)
-    g.sync.wait_ge(s.dgt, 16)
-    g.sync.dma_start(T.y[0:64, col(rank + 2)], T.dg[0:2]).then_inc(s.stored, 16)
+    g.sync.wait_ge(s.nswd, 2)
+    g.sync.dma_start(T.y[96:128, col(sw)], T.nsw[3]).then_inc(s.stored, 16)
+    g.sync.wait_ge(s.nswf, 24)
+    g.sync.dma_start(T.y[0:96, col(sw)], T.nsw[0:3]).then_inc(s.stored, 16)
+    g.sync.wait_ge(s.dga, 24)
+    g.sync.dma_start(T.y[0:96, col(dgr)], T.dg[0:3]).then_inc(s.stored, 16)
 
     g.scalar.wait_ge(s.sent, 16)
     g.scalar.dma_start(T.y[:, col(rank)], T.x[:]).then_inc(s.stored, 16)
-    g.scalar.wait_ge(s.nbrd, 4)
-    g.scalar.dma_start(T.y[0:64, col(rank + 1)], T.nbr[0:2]).then_inc(s.stored, 16)
-    g.scalar.wait_ge(s.nbrf, 16)
-    g.scalar.dma_start(T.y[64:128, col(rank + 1)], T.nbr[2:4]).then_inc(s.stored, 16)
-    g.scalar.wait_ge(s.dgb, 16)
-    g.scalar.dma_start(T.y[64:128, col(rank + 2)], T.dg[2:4]).then_inc(s.stored, 16)
+    g.scalar.wait_ge(s.ncbf, 8)
+    g.scalar.dma_start(T.y[96:128, col(cb)], T.ncb[3]).then_inc(s.stored, 16)
+    g.scalar.wait_ge(s.dgb, 8)
+    g.scalar.dma_start(T.y[96:128, col(dgr)], T.dg[3]).then_inc(s.stored, 16)
+    g.scalar.wait_ge(s.ncbd, 6)
+    g.scalar.dma_start(T.y[0:96, col(cb)], T.ncb[0:3]).then_inc(s.stored, 16)
 
     g.wait_ge(s.sent, 16)
     g.wait_ge(s.stored, 112)

@@ -11,6 +11,7 @@ SEMAPHORES = ["loaded", "sent", "relay", "nswd", "nswf", "ncbd", "ncbf", "dga", 
 
 CABLE_FWD = (4, 6, 0)
 SWITCH_FWD = 5
+CABLE_OUT = {1: 1, 7: 2}
 W = 64
 
 
@@ -42,25 +43,29 @@ def rank_program(g, core, T, topo):
             return
         sw, cb = neighbours(q)
         loc = core % 8
-        g_calls = None
         if loc in CABLE_FWD:
             p = CABLE_FWD.index(loc)
-            g_calls = [tr(cores[cb], 0x00FF, s.dga, T.relay[:], T.dg[p]),
-                       tr(cores[q], 0xFF00, s.nswf, T.relay[:], T.nsw[p])]
+            need = 2
+            calls = [tr(cores[cb], 0x00FF, s.dga, T.relay[:], T.dg[p]),
+                     tr(cores[q], 0xFF00, s.nswf, T.relay[:], T.nsw[p])]
         elif loc == SWITCH_FWD:
-            g_calls = [tr(cores[sw], 0x00FF, s.dgb, T.relay[:], T.dg[3]),
-                       tr(cores[q], 0xFF00, s.ncbf, T.relay[:], T.ncb[3])]
-        if g_calls is None:
+            need = 2
+            calls = [tr(cores[sw], 0x00FF, s.dgb, T.relay[:], T.dg[3]),
+                     tr(cores[q], 0xFF00, s.ncbf, T.relay[:], T.ncb[3])]
+        elif loc in CABLE_OUT:
+            need = 4
+            calls = [tr(cores[cb], 0x00FF, s.ncbd, T.relay[:], T.ncb[CABLE_OUT[loc]])]
+        else:
             return
-        g.wait_ge(s.relay, 2)
-        g.remote_dma_fused(g_calls, local_sem=s.sent)
-        g.wait_ge(s.sent, 16)
+        g.wait_ge(s.relay, need)
+        g.remote_dma_fused(calls, local_sem=s.sent)
+        g.wait_ge(s.sent, 8 * len(calls))
         return
 
     sw, cb = neighbours(rank)
     dgr = (rank + 2) % n
     csw, ccb = cores[sw], cores[cb]
-    bsw, bcb = csw - csw % 8, ccb - ccb % 8
+    bsw, bcb, bme = csw - csw % 8, ccb - ccb % 8, core - core % 8
 
     def col(j):
         return slice(W * j, W * j + W)
@@ -69,33 +74,33 @@ def rank_program(g, core, T, topo):
     g.wait_ge(s.loaded, 16)
 
     g.remote_dma_fused([
-        tr(bsw + CABLE_FWD[0], 0x03, s.relay, T.own[0], T.relay[:]),
-        tr(bsw + CABLE_FWD[1], 0x0C, s.relay, T.own[1], T.relay[:]),
-        tr(bsw + CABLE_FWD[2], 0x30, s.relay, T.own[2], T.relay[:]),
-        tr(bcb + SWITCH_FWD, 0xC0, s.relay, T.own[3], T.relay[:]),
+        tr(bsw + CABLE_FWD[0], 0x0003, s.relay, T.own[0], T.relay[:]),
+        tr(bsw + CABLE_FWD[1], 0x000C, s.relay, T.own[1], T.relay[:]),
+        tr(bsw + CABLE_FWD[2], 0x0030, s.relay, T.own[2], T.relay[:]),
+        tr(bcb + SWITCH_FWD, 0x00C0, s.relay, T.own[3], T.relay[:]),
+        tr(bme + 1, 0x0F00, s.relay, T.own[CABLE_OUT[1]], T.relay[:]),
+        tr(bme + 7, 0xF000, s.relay, T.own[CABLE_OUT[7]], T.relay[:]),
     ], local_sem=s.sent)
     g.remote_dma_fused([
-        tr(ccb, 0x03, s.ncbd, T.own[0], T.ncb[0]),
-        tr(ccb, 0x0C, s.ncbd, T.own[1], T.ncb[1]),
-        tr(ccb, 0x30, s.ncbd, T.own[2], T.ncb[2]),
-        tr(csw, 0xC0, s.nswd, T.own[3], T.nsw[3]),
+        tr(ccb, 0x0F, s.ncbd, T.own[0], T.ncb[0]),
+        tr(csw, 0xF0, s.nswd, T.own[3], T.nsw[3]),
     ], local_sem=s.sent)
 
-    g.sync.wait_ge(s.nswd, 2)
+    g.sync.wait_ge(s.nswd, 4)
     g.sync.dma_start(T.y[96:128, col(sw)], T.nsw[3]).then_inc(s.stored, 16)
     g.sync.wait_ge(s.nswf, 24)
     g.sync.dma_start(T.y[0:96, col(sw)], T.nsw[0:3]).then_inc(s.stored, 16)
     g.sync.wait_ge(s.dga, 24)
     g.sync.dma_start(T.y[0:96, col(dgr)], T.dg[0:3]).then_inc(s.stored, 16)
 
-    g.scalar.wait_ge(s.sent, 16)
+    g.scalar.wait_ge(s.sent, 24)
     g.scalar.dma_start(T.y[:, col(rank)], T.x[:]).then_inc(s.stored, 16)
+    g.scalar.wait_ge(s.ncbd, 20)
+    g.scalar.dma_start(T.y[0:96, col(cb)], T.ncb[0:3]).then_inc(s.stored, 16)
     g.scalar.wait_ge(s.ncbf, 8)
     g.scalar.dma_start(T.y[96:128, col(cb)], T.ncb[3]).then_inc(s.stored, 16)
     g.scalar.wait_ge(s.dgb, 8)
     g.scalar.dma_start(T.y[96:128, col(dgr)], T.dg[3]).then_inc(s.stored, 16)
-    g.scalar.wait_ge(s.ncbd, 6)
-    g.scalar.dma_start(T.y[0:96, col(cb)], T.ncb[0:3]).then_inc(s.stored, 16)
 
-    g.wait_ge(s.sent, 16)
+    g.wait_ge(s.sent, 24)
     g.wait_ge(s.stored, 112)

from concourse.bass import DstId, RemoteDMATransfer

SCRATCH = {
    "own": ("dram", [4, 128, 16], "float32"),
    "relay": ("dram", [128, 16], "float32"),
    "nsw": ("dram", [4, 128, 16], "float32"),
    "ncb": ("dram", [4, 128, 16], "float32"),
    "dg": ("dram", [4, 128, 16], "float32"),
}
SEMAPHORES = ["loaded", "sent", "relay", "nswd", "nswf", "ncbd", "ncbf", "dga", "dgb", "stored"]

CABLE_FWD = (4, 6, 0)
SWITCH_FWD = 5
CABLE_OUT = {1: 1, 7: 2}
W = 64


def rank_program(g, core, T, topo):
    cores = list(T.cores)
    n = len(cores)
    s = T.sem
    rank = T.rank_of(core)

    def did(dst):
        rid, pid = topo.addr(dst, core)
        return DstId(rid=rid, pnc=pid)

    def tr(dst, mask, sem, src, out):
        return RemoteDMATransfer(dst_ids=[did(dst)], dma_engine_mask=mask, remote_sem=sem, src=src, dst=out)

    def neighbours(q):
        a, b = (q + 1) % n, (q - 1) % n
        if topo.rack(topo.host(cores[a])) == topo.rack(topo.host(cores[q])):
            return a, b
        return b, a

    if rank is None:
        q = None
        for i in range(n):
            if cores[i] // 8 == core // 8:
                q = i
        if q is None:
            return
        sw, cb = neighbours(q)
        loc = core % 8
        if loc in CABLE_FWD:
            p = CABLE_FWD.index(loc)
            need = 2
            calls = [tr(cores[cb], 0x00FF, s.dga, T.relay[:], T.dg[p]),
                     tr(cores[q], 0xFF00, s.nswf, T.relay[:], T.nsw[p])]
        elif loc == SWITCH_FWD:
            need = 2
            calls = [tr(cores[sw], 0x00FF, s.dgb, T.relay[:], T.dg[3]),
                     tr(cores[q], 0xFF00, s.ncbf, T.relay[:], T.ncb[3])]
        elif loc in CABLE_OUT:
            need = 4
            calls = [tr(cores[cb], 0x00FF, s.ncbd, T.relay[:], T.ncb[CABLE_OUT[loc]])]
        else:
            return
        g.wait_ge(s.relay, need)
        g.remote_dma_fused(calls, local_sem=s.sent)
        g.wait_ge(s.sent, 8 * len(calls))
        return

    sw, cb = neighbours(rank)
    dgr = (rank + 2) % n
    csw, ccb = cores[sw], cores[cb]
    bsw, bcb, bme = csw - csw % 8, ccb - ccb % 8, core - core % 8

    def col(j):
        return slice(W * j, W * j + W)

    g.sync.dma_start(T.own[:], T.x[:]).then_inc(s.loaded, 16)
    g.wait_ge(s.loaded, 16)

    g.remote_dma_fused([
        tr(bsw + CABLE_FWD[0], 0x0003, s.relay, T.own[0], T.relay[:]),
        tr(bsw + CABLE_FWD[1], 0x000C, s.relay, T.own[1], T.relay[:]),
        tr(bsw + CABLE_FWD[2], 0x0030, s.relay, T.own[2], T.relay[:]),
        tr(bcb + SWITCH_FWD, 0x00C0, s.relay, T.own[3], T.relay[:]),
        tr(bme + 1, 0x0F00, s.relay, T.own[CABLE_OUT[1]], T.relay[:]),
        tr(bme + 7, 0xF000, s.relay, T.own[CABLE_OUT[7]], T.relay[:]),
    ], local_sem=s.sent)
    g.remote_dma_fused([
        tr(ccb, 0x0F, s.ncbd, T.own[0], T.ncb[0]),
        tr(csw, 0xF0, s.nswd, T.own[3], T.nsw[3]),
    ], local_sem=s.sent)

    g.sync.wait_ge(s.nswd, 4)
    g.sync.dma_start(T.y[96:128, col(sw)], T.nsw[3]).then_inc(s.stored, 16)
    g.sync.wait_ge(s.nswf, 24)
    g.sync.dma_start(T.y[0:96, col(sw)], T.nsw[0:3]).then_inc(s.stored, 16)
    g.sync.wait_ge(s.dga, 24)
    g.sync.dma_start(T.y[0:96, col(dgr)], T.dg[0:3]).then_inc(s.stored, 16)

    g.scalar.wait_ge(s.sent, 24)
    g.scalar.dma_start(T.y[:, col(rank)], T.x[:]).then_inc(s.stored, 16)
    g.scalar.wait_ge(s.ncbd, 20)
    g.scalar.dma_start(T.y[0:96, col(cb)], T.ncb[0:3]).then_inc(s.stored, 16)
    g.scalar.wait_ge(s.ncbf, 8)
    g.scalar.dma_start(T.y[96:128, col(cb)], T.ncb[3]).then_inc(s.stored, 16)
    g.scalar.wait_ge(s.dgb, 8)
    g.scalar.dma_start(T.y[96:128, col(dgr)], T.dg[3]).then_inc(s.stored, 16)

    g.wait_ge(s.sent, 24)
    g.wait_ge(s.stored, 112)
